import numpy as np
import ml_dtypes


def mxq(x, axis, fmt="e4m3"):
    dtype, down = {"e4m3": (ml_dtypes.float8_e4m3fn, 7), "e5m2": (ml_dtypes.float8_e5m2, 14)}[fmt]
    v = np.moveaxis(np.asarray(x, np.float32).astype(ml_dtypes.bfloat16).astype(np.float64), axis, -1)
    blocks = v.reshape(v.shape[:-1] + (-1, 32))
    amax = np.abs(blocks).max(-1, keepdims=True)
    byte = np.maximum(np.where(amax > 0, np.frexp(amax)[1] - 1 + 127, 0) - down, 1)
    scale = np.exp2(byte - 127.0)
    codes = (blocks / scale).astype(np.float32).astype(dtype).astype(np.float64)
    return np.moveaxis((codes * scale).reshape(v.shape), -1, axis)


WIDE = False


def mx_kscale(k):
    if not WIDE:
        return np.ones(k)
    levels = np.array([10, -10, 5, -5, 0])
    if k % 512:
        return np.exp2(np.random.permutation(np.resize(levels, k // 32))).repeat(32)
    a = np.empty((k // 512, 16))
    for p in range(k // 512):
        a[p, :8] = np.random.permutation(np.resize(levels, 8))
        for g in range(8):
            far = levels[np.abs(levels - a[p, g]) >= 10]
            a[p, g + 8] = far[np.random.randint(len(far))]
    return np.exp2(a.ravel()).repeat(32)


def f64(x):
    return np.asarray(x).astype(np.float64)


def striped(idx):
    return np.tile(idx.reshape(-1, 16).T, (8, 1)).astype(np.uint16)


def unstriped(offs):
    return offs[:16].T.reshape(-1).astype(np.int64)


E2M1 = np.array([0.0, 0.5, 1.0, 1.5, 2.0, 3.0, 4.0, 6.0, -0.0, -0.5, -1.0, -1.5, -2.0, -3.0, -4.0, -6.0])


def pack_weight(w, fmt):
    k, n = w.shape
    w = f64(np.asarray(w, np.float32).astype(ml_dtypes.bfloat16)).reshape(k // 32, 32, n)
    amax = np.abs(w).max(1)
    if fmt == "e4m3":
        byte = np.frexp(amax)[1] - 1 + 127 - 7
    else:
        mant, ex = np.frexp(amax / 6.0)
        byte = np.where(mant > 0.5, ex, ex - 1) + 127
    byte = np.clip(np.where(amax > 0, byte, 1), 1, 254)
    scaled = (w * np.exp2(127.0 - byte)[:, None, :]).reshape(k, n).astype(np.float32)
    by_word = np.ascontiguousarray(scaled.reshape(k // 512, 128, 4, n).transpose(0, 1, 3, 2))
    if fmt == "e4m3":
        words = by_word.astype(ml_dtypes.float8_e4m3fn).view(np.uint8)
    else:
        c = by_word.astype(ml_dtypes.float4_e2m1fn).view(np.uint8) & 0xF
        words = (c[..., 0::2] | (c[..., 1::2] << 4)).reshape(k // 512, 128, 2 * n)
    return np.ascontiguousarray(words), np.ascontiguousarray(byte.astype(np.uint8).reshape(k // 512, 16, n))


def unpack_weight(words, scales, fmt):
    g, _, n = scales.shape
    words = np.ascontiguousarray(words).reshape(g, 128, n, -1)
    if fmt == "e4m3":
        vals = words.view(ml_dtypes.float8_e4m3fn).astype(np.float64)
    else:
        nib = np.empty((g, 128, n, 4), np.uint8)
        nib[..., 0::2] = words & 0xF
        nib[..., 1::2] = words >> 4
        vals = E2M1[nib]
    vals = vals * np.repeat(np.exp2(scales.astype(np.float64) - 127.0), 8, axis=1)[..., None]
    return vals.transpose(0, 1, 3, 2).reshape(g * 512, n)


def relu(v):
    return np.maximum(v, 0.0)


K, T, E, C, H, N = 512, 640, 4, 128, 512, 256


def by_expert(wq, xq):
    return np.concatenate([wq[e].T @ xq[:, e * C:(e + 1) * C] for e in range(E)], axis=1)


def setup_inputs():
    n = np.random.standard_normal
    s = mx_kscale(K)[:, None]
    u = mx_kscale(H)
    w1 = [pack_weight(m, "e2m1") for m in n((E + 1, K, H)) / np.sqrt(K) / s[None]]
    w3 = [pack_weight(m, "e2m1") for m in n((E + 1, K, H)) / np.sqrt(K) / s[None] * u[None, None, :]]
    w2 = [pack_weight(m, "e2m1") for m in n((E + 1, H, N)) / np.sqrt(H) / u[None, :, None]]
    return {
        "xT": (n((K, T)) * s).astype(np.float32),
        "w1_words": np.stack([m[0] for m in w1]),
        "w1_scales": np.stack([m[1] for m in w1]),
        "w3_words": np.stack([m[0] for m in w3]),
        "w3_scales": np.stack([m[1] for m in w3]),
        "w2_words": np.stack([m[0] for m in w2]),
        "w2_scales": np.stack([m[1] for m in w2]),
        "gate": np.tile(np.random.uniform(0.2, 1.0, E * C), (N, 1)).astype(np.float32),
        "offs": striped(np.random.permutation(T)[:E * C]),
    }


def reference(xT, w1_words, w1_scales, w3_words, w3_scales, w2_words, w2_scales, gate, offs):
    idx = unstriped(offs)
    w1 = np.stack([unpack_weight(w1_words[e], w1_scales[e], "e2m1") for e in range(E + 1)])
    w3 = np.stack([unpack_weight(w3_words[e], w3_scales[e], "e2m1") for e in range(E + 1)])
    w2 = np.stack([unpack_weight(w2_words[e], w2_scales[e], "e2m1") for e in range(E + 1)])
    w1q, w3q, w2q = w1, w3, w2
    xs = mxq(f64(xT), 0, "e4m3")
    hs = relu(w1q[E].T @ xs) * (w3q[E].T @ xs)
    ys = w2q[E].T @ mxq(hs, 0, "e4m3")
    xq = mxq(f64(xT)[:, idx], 0, "e4m3")
    h = relu(by_expert(w1q, xq))
    h = h * by_expert(w3q, xq)
    y = by_expert(w2q, mxq(h, 0, "e4m3"))
    out = ys
    out[:, idx] += f64(gate) * y
    return out

@@ -1,0 +1,274 @@
+from contextlib import ExitStack
+
+import concourse.mybir as mybir
+from concourse.masks import make_identity
+
+FLOPS = 1509949440
+
+K, T, E, C, H, N = 512, 640, 4, 128, 512, 256
+S = E * C
+SHARED = E
+P = 128
+HALVES = N // P
+
+F32 = mybir.dt.float32
+BF16 = mybir.dt.bfloat16
+I32 = mybir.dt.int32
+U32 = mybir.dt.uint32
+U16 = mybir.dt.uint16
+U8 = mybir.dt.uint8
+FP8X4 = mybir.dt.float8_e4m3fn_x4
+FP4X4 = mybir.dt.float4_e2m1fn_x4
+RELU = mybir.ActivationFunctionType.Relu
+MULT = mybir.AluOpType.mult
+ADD = mybir.AluOpType.add
+
+X_SPLIT = 256
+
+
+def tile_moe_shr_glu_relu_kernel(
+    tc, xT, w1_words, w1_scales, w3_words, w3_scales, w2_words, w2_scales, gate, offs, out
+):
+    nc = tc.nc
+    with ExitStack() as ctx:
+        keep = ctx.enter_context(tc.tile_pool(name="keep", bufs=1))
+        work = ctx.enter_context(tc.tile_pool(name="work", bufs=3))
+        psum = ctx.enter_context(tc.psum_pool(name="psum", bufs=2))
+
+        offsets = keep.tile([P, S // 16], U16, name="offsets")
+        x_a = keep.tile([P, 4, X_SPLIT], F32, name="x_a")
+        x_b = keep.tile([P, 4, T - X_SPLIT], F32, name="x_b")
+        w1 = keep.tile([P, E + 1, 2 * H], U8, name="w1", align_bytes=64)
+        w3 = keep.tile([P, E + 1, 2 * H], U8, name="w3", align_bytes=64)
+        w2 = keep.tile([P, E + 1, 2 * N], U8, name="w2", align_bytes=64)
+        s1 = keep.tile([P, E + 1, H], U8, name="s1", align_bytes=64)
+        s3 = keep.tile([P, E + 1, H], U8, name="s3", align_bytes=64)
+        s2 = keep.tile([P, E + 1, N], U8, name="s2", align_bytes=64)
+        gates = keep.tile([P, HALVES, S], F32, name="gates")
+        ident = keep.tile([P, P], F32, name="ident")
+        warm = keep.tile([P, 1], F32, name="warm")
+        pairs = [keep.tile([P, T], U32, name=f"pairs{u}") for u in range(2)]
+        x_in = keep.tile([P, T, 4], BF16, name="x_in", align_bytes=64)
+        x_codes = keep.tile([P, T], U32, name="x_codes", align_bytes=64)
+        x_scales = keep.tile([P, T], U8, name="x_scales", align_bytes=64)
+        g_codes = keep.tile([P, S], U32, name="g_codes", align_bytes=64)
+        g_scales = keep.tile([P, S], U8, name="g_scales", align_bytes=64)
+        hs_codes = keep.tile([P, T], U32, name="hs_codes", align_bytes=64)
+        hs_scales = keep.tile([P, T], U8, name="hs_scales", align_bytes=64)
+        windows = [keep.tile([P, T], F32, name=f"window{h}") for h in range(HALVES)]
+        results = [keep.tile([P, T], F32, name=f"result{h}") for h in range(HALVES)]
+
+        x_rows = xT.rearrange("(p j) t -> p j t", j=4)
+
+        def load_words(eng, tile, words, e0, e1):
+            eng.dma_start(
+                out=tile[:, e0:e1, :].bitcast(I32),
+                in_=words[e0:e1, 0].rearrange("e p b -> p e b").bitcast(I32),
+            )
+
+        def load_scales(eng, tile, scales, r):
+            rows = scales[:, 0].rearrange("e (q r) c -> r q e c", r=4)
+            eng.dma_start(out=tile[r:P:32, :, :].bitcast(I32), in_=rows[r].bitcast(I32))
+
+        def zero_plane(eng, tile):
+            eng.memset(tile[:].rearrange("p e c -> p (e c)").bitcast(I32), 0)
+
+        def touch(words):
+            nc.gpsimd.memset(words.bitcast(I32), 0)
+
+        nc.sync.dma_start(out=x_a[:], in_=x_rows[:, :, :X_SPLIT])
+        load_words(nc.sync, w1, w1_words, SHARED, SHARED + 1)
+        nc.sync.dma_start(offsets[:], offs)
+        zero_plane(nc.gpsimd, s1)
+        for r in range(4):
+            load_scales(nc.sync, s1, w1_scales, r)
+        touch(x_b[:, 0, 0:1])
+        nc.sync.dma_start(out=x_b[:], in_=x_rows[:, :, X_SPLIT:])
+        touch(w3[:, SHARED, 0:4])
+        load_words(nc.sync, w3, w3_words, SHARED, SHARED + 1)
+        zero_plane(nc.gpsimd, s3)
+        for r in range(4):
+            load_scales(nc.sync, s3, w3_scales, r)
+        touch(w1[:, 0, 0:4])
+        load_words(nc.sync, w1, w1_words, 0, E)
+        touch(w3[:, 0, 0:4])
+        load_words(nc.sync, w3, w3_words, 0, E)
+        zero_plane(nc.gpsimd, s2)
+        for r in range(4):
+            load_scales(nc.sync, s2, w2_scales, r)
+        touch(w2[:, 0, 0:4])
+        load_words(nc.sync, w2, w2_words, 0, E + 1)
+        touch(gates[:, 0, 0:1])
+        nc.sync.dma_start(out=gates[:], in_=gate.rearrange("(h p) s -> p h s", p=P))
+        make_identity(nc, ident[:])
+        nc.vector.memset(warm[:], 0.0)
+        nc.scalar.activation(warm[:], warm[:], RELU)
+        for h in range(HALVES):
+            nc.vector.memset(windows[h][:], 0.0)
+
+        def x_part(t0, t1):
+            return x_a[:, :, t0:t1] if t1 <= X_SPLIT else x_b[:, :, t0 - X_SPLIT : t1 - X_SPLIT]
+
+        def cast_shared(t0, t1):
+            nc.vector.tensor_copy(out=x_in[:, t0:t1, :], in_=x_part(t0, t1).rearrange("p j t -> p t j"))
+            nc.vector.quantize_mx(
+                out=x_codes[:, t0:t1].bitcast(FP8X4),
+                scales=x_scales[:, t0:t1],
+                in_=x_in[:, t0:t1, :].rearrange("p t j -> p (t j)"),
+            )
+
+        def cast_pairs(eng_copy, t0, t1):
+            for u in range(2):
+                eng_copy(
+                    out=pairs[u][:, t0:t1].bitcast(BF16).rearrange("p (t d) -> p t d", d=2),
+                    in_=x_part(t0, t1)[:, 2 * u : 2 * u + 2, :].rearrange("p d t -> p t d"),
+                )
+
+        def gather(j0, j1):
+            grouped = work.tile([P, j1 - j0, 2], U32, name="grouped", align_bytes=64)
+            for u in range(2):
+                nc.vector.tensor_copy(
+                    out=grouped[:, :, u], in_=pairs[u][:].indirect(offsets[:, j0 // 16 : j1 // 16])
+                )
+            nc.vector.quantize_mx(
+                out=g_codes[:, j0:j1].bitcast(FP8X4),
+                scales=g_scales[:, j0:j1],
+                in_=grouped[:].rearrange("p s u -> p (s u)").bitcast(BF16),
+            )
+
+        def layer1(e, codes, scales, cols):
+            sums = []
+            for tag, words, planes in (("a", w1, s1), ("b", w3, s3)):
+                bank = psum.tile([P, H], F32, name=f"bank_{tag}", tag=tag)
+                nc.tensor.matmul_mx(
+                    out=bank[:],
+                    lhsT=codes[:, cols].bitcast(FP8X4),
+                    lhsT_scale=scales[:, cols],
+                    rhs=words[:, e, :].bitcast(FP4X4),
+                    rhs_scale=planes[:, e, :],
+                    start=True,
+                    stop=True,
+                )
+                sums.append(bank)
+            positive = work.tile([P, H], F32, name="positive")
+            nc.scalar.activation(positive[:], sums[0][:], RELU)
+            hidden = work.tile([P, H], BF16, name="hidden", align_bytes=64)
+            nc.vector.tensor_tensor(hidden[:], sums[1][:], positive[:], MULT)
+            return hidden
+
+        def turn(group):
+            n = len(group)
+            bank = psum.tile([P, n, 2, P], F32, name="bank_t", tag="t")
+            for i, hidden in enumerate(group):
+                words = hidden[:].bitcast(F32)
+                for u in range(2):
+                    nc.tensor.transpose(bank[:, i, u, :], words[:, u::2], ident[:])
+            turned = work.tile([P, n, P, 2], F32, name="turned", align_bytes=64)
+            nc.scalar.copy(out=turned[:], in_=bank[:].rearrange("p i u r -> p i r u"))
+            return turned
+
+        def quantize_hidden(turned, codes, scales):
+            nc.vector.quantize_mx(
+                out=codes.bitcast(FP8X4),
+                scales=scales,
+                in_=turned[:].rearrange("p i r u -> p (i r u)").bitcast(BF16),
+            )
+
+        def layer2(e, h, bank, codes, scales):
+            nc.tensor.matmul_mx(
+                out=bank,
+                lhsT=w2[:, e, 2 * P * h : 2 * P * (h + 1)].bitcast(FP4X4),
+                lhsT_scale=s2[:, e, P * h : P * (h + 1)],
+                rhs=codes.bitcast(FP8X4),
+                rhs_scale=scales,
+                start=True,
+                stop=True,
+            )
+
+        def experts_out(e0, n, turned):
+            codes = work.tile([P, n, C], U32, name="h_codes", align_bytes=64)
+            scales = work.tile([P, n, C], U8, name="h_scales", align_bytes=64)
+            quantize_hidden(turned, codes[:].rearrange("p n c -> p (n c)"), scales[:].rearrange("p n c -> p (n c)"))
+            bank = psum.tile([P, HALVES, n * C], F32, name="bank_y", tag="y")
+            for i in range(n):
+                for h in range(HALVES):
+                    layer2(e0 + i, h, bank[:, h, i * C : (i + 1) * C], codes[:, i, :], scales[:, i, :])
+            y = work.tile([P, HALVES, n * C], F32, name="y", bufs=4)
+            nc.scalar.copy(out=y[:], in_=bank[:])
+            return y
+
+        def scatter(e0, n, h, y):
+            nc.vector.tensor_tensor(
+                windows[h][:].indirect(offsets[:, e0 * C // 16 : (e0 + n) * C // 16]),
+                y[:, h, :],
+                gates[:, h, e0 * C : (e0 + n) * C],
+                MULT,
+            )
+
+        def cols(i, n=1):
+            return slice(i * P, (i + n) * P)
+
+        chunks = T // P
+        groups = [(0, 2), (2, 2), (4, 1), (5, 2), (7, 1), (8, 1)]
+        hidden = {}
+        turned = {}
+        ys = {}
+        total = chunks + E
+
+        def chunk_step(c):
+            if c < chunks:
+                hidden[c] = layer1(SHARED, x_codes, x_scales, cols(c))
+            else:
+                hidden[c] = layer1(c - chunks, g_codes, g_scales, cols(c - chunks))
+
+        def finish(g):
+            c, n = groups[g]
+            if c < chunks:
+                quantize_hidden(turned[g], hs_codes[:, cols(c, n)], hs_scales[:, cols(c, n)])
+            else:
+                ys[g] = experts_out(c - chunks, n, turned[g])
+
+        cast_shared(0, 256)
+        chunk_step(0)
+        cast_pairs(nc.scalar.copy, 0, 256)
+        cast_shared(256, 512)
+        cast_shared(512, 640)
+        chunk_step(1)
+        cast_pairs(nc.scalar.copy, 256, 640)
+        turned[0] = turn([hidden[0], hidden[1]])
+        chunk_step(2)
+        gather(0, 256)
+        finish(0)
+        chunk_step(3)
+        turned[1] = turn([hidden[2], hidden[3]])
+        chunk_step(4)
+        finish(1)
+        gather(256, 512)
+        turned[2] = turn([hidden[4]])
+        chunk_step(5)
+        finish(2)
+        chunk_step(6)
+        turned[3] = turn([hidden[5], hidden[6]])
+        chunk_step(7)
+        finish(3)
+        turned[4] = turn([hidden[7]])
+        chunk_step(8)
+        scatter(0, 2, 0, ys[3])
+        finish(4)
+        turned[5] = turn([hidden[8]])
+        finish(5)
+        scatter(0, 2, 1, ys[3])
+
+        tail = psum.tile([P, HALVES, P], F32, name="bank_tail", tag="a")
+        bodies = []
+        for h in range(HALVES):
+            body = psum.tile([P, 512], F32, name="bank_body", tag="b")
+            layer2(SHARED, h, body[:], hs_codes[:, 0:512], hs_scales[:, 0:512])
+            layer2(SHARED, h, tail[:, h, :], hs_codes[:, 512:640], hs_scales[:, 512:640])
+            bodies.append(body)
+        for h in range(HALVES):
+            scatter(2, 1, h, ys[4])
+            scatter(3, 1, h, ys[5])
+            for bank, t0, t1 in ((bodies[h][:], 0, 512), (tail[:, h, :], 512, 640)):
+                nc.vector.tensor_tensor(results[h][:, t0:t1], bank, windows[h][:, t0:t1], ADD)
+                nc.sync.dma_start(out=out[h * P : (h + 1) * P, t0:t1], in_=results[h][:, t0:t1])

@@ -32,7 +32,7 @@ def tile_moe_shr_glu_relu_kernel(
     nc = tc.nc
     with ExitStack() as ctx:
         keep = ctx.enter_context(tc.tile_pool(name="keep", bufs=1))
-        work = ctx.enter_context(tc.tile_pool(name="work", bufs=3))
+        work = ctx.enter_context(tc.tile_pool(name="work", bufs=6))
         psum = ctx.enter_context(tc.psum_pool(name="psum", bufs=2))
 
         offsets = keep.tile([P, S // 16], U16, name="offsets")
@@ -109,20 +109,24 @@ def tile_moe_shr_glu_relu_kernel(
         def x_part(t0, t1):
             return x_a[:, :, t0:t1] if t1 <= X_SPLIT else x_b[:, :, t0 - X_SPLIT : t1 - X_SPLIT]
 
-        def cast_shared(t0, t1):
-            nc.vector.tensor_copy(out=x_in[:, t0:t1, :], in_=x_part(t0, t1).rearrange("p j t -> p t j"))
+        def lay_shared(eng_copy, t0, t1):
+            eng_copy(out=x_in[:, t0:t1, :], in_=x_part(t0, t1).rearrange("p j t -> p t j"))
+
+        def quantize_shared(t0, t1):
             nc.vector.quantize_mx(
                 out=x_codes[:, t0:t1].bitcast(FP8X4),
                 scales=x_scales[:, t0:t1],
                 in_=x_in[:, t0:t1, :].rearrange("p t j -> p (t j)"),
             )
 
-        def cast_pairs(eng_copy, t0, t1):
-            for u in range(2):
-                eng_copy(
-                    out=pairs[u][:, t0:t1].bitcast(BF16).rearrange("p (t d) -> p t d", d=2),
-                    in_=x_part(t0, t1)[:, 2 * u : 2 * u + 2, :].rearrange("p d t -> p t d"),
-                )
+        def gpsimd_copy(out, in_):
+            nc.gpsimd.tensor_scalar(out, in_, 1.0, 0.0, MULT, ADD)
+
+        def cast_pairs(copy, u, t0, t1):
+            copy(
+                out=pairs[u][:, t0:t1].bitcast(BF16).rearrange("p (t d) -> p t d", d=2),
+                in_=x_part(t0, t1)[:, 2 * u : 2 * u + 2, :].rearrange("p d t -> p t d"),
+            )
 
         def gather(j0, j1):
             grouped = work.tile([P, j1 - j0, 2], U32, name="grouped", align_bytes=64)
@@ -193,7 +197,7 @@ def tile_moe_shr_glu_relu_kernel(
             for i in range(n):
                 for h in range(HALVES):
                     layer2(e0 + i, h, bank[:, h, i * C : (i + 1) * C], codes[:, i, :], scales[:, i, :])
-            y = work.tile([P, HALVES, n * C], F32, name="y", bufs=4)
+            y = work.tile([P, HALVES, n * C], F32, name="y")
             nc.scalar.copy(out=y[:], in_=bank[:])
             return y
 
@@ -209,7 +213,7 @@ def tile_moe_shr_glu_relu_kernel(
             return slice(i * P, (i + n) * P)
 
         chunks = T // P
-        groups = [(0, 2), (2, 2), (4, 1), (5, 2), (7, 1), (8, 1)]
+        groups = [(0, 2), (2, 2), (4, 1), (5, 2), (7, 2)]
         hidden = {}
         turned = {}
         ys = {}
@@ -228,37 +232,38 @@ def tile_moe_shr_glu_relu_kernel(
             else:
                 ys[g] = experts_out(c - chunks, n, turned[g])
 
-        cast_shared(0, 256)
-        chunk_step(0)
-        cast_pairs(nc.scalar.copy, 0, 256)
-        cast_shared(256, 512)
-        cast_shared(512, 640)
-        chunk_step(1)
-        cast_pairs(nc.scalar.copy, 256, 640)
-        turned[0] = turn([hidden[0], hidden[1]])
-        chunk_step(2)
+        lay_shared(nc.vector.tensor_copy, 0, 128)
+        lay_shared(nc.vector.tensor_copy, 128, 256)
+        quantize_shared(0, 128)
+        quantize_shared(128, 256)
+        cast_pairs(nc.scalar.copy, 0, 0, 256)
+        cast_pairs(nc.scalar.copy, 1, 0, 256)
+        cast_pairs(nc.scalar.copy, 0, 256, 640)
+        cast_pairs(nc.vector.tensor_copy, 1, 256, 640)
+        lay_shared(nc.vector.tensor_copy, 256, 640)
         gather(0, 256)
+        gather(256, 512)
+        quantize_shared(256, 512)
+        quantize_shared(512, 640)
+        chunk_step(0)
+        chunk_step(1)
+        chunk_step(5)
+        chunk_step(6)
+        turned[0] = turn([hidden[0], hidden[1]])
+        turned[3] = turn([hidden[5], hidden[6]])
+        chunk_step(7)
+        chunk_step(8)
+        finish(3)
         finish(0)
+        turned[4] = turn([hidden[7], hidden[8]])
+        finish(4)
+        chunk_step(2)
         chunk_step(3)
         turned[1] = turn([hidden[2], hidden[3]])
         chunk_step(4)
-        finish(1)
-        gather(256, 512)
         turned[2] = turn([hidden[4]])
-        chunk_step(5)
+        finish(1)
         finish(2)
-        chunk_step(6)
-        turned[3] = turn([hidden[5], hidden[6]])
-        chunk_step(7)
-        finish(3)
-        turned[4] = turn([hidden[7]])
-        chunk_step(8)
-        scatter(0, 2, 0, ys[3])
-        finish(4)
-        turned[5] = turn([hidden[8]])
-        finish(5)
-        scatter(0, 2, 1, ys[3])
-
         tail = psum.tile([P, HALVES, P], F32, name="bank_tail", tag="a")
         bodies = []
         for h in range(HALVES):
@@ -267,8 +272,8 @@ def tile_moe_shr_glu_relu_kernel(
             layer2(SHARED, h, tail[:, h, :], hs_codes[:, 512:640], hs_scales[:, 512:640])
             bodies.append(body)
         for h in range(HALVES):
-            scatter(2, 1, h, ys[4])
-            scatter(3, 1, h, ys[5])
+            scatter(0, 2, h, ys[3])
+            scatter(2, 2, h, ys[4])
             for bank, t0, t1 in ((bodies[h][:], 0, 512), (tail[:, h, :], 512, 640)):
                 nc.vector.tensor_tensor(results[h][:, t0:t1], bank, windows[h][:, t0:t1], ADD)
                 nc.sync.dma_start(out=out[h * P : (h + 1) * P, t0:t1], in_=results[h][:, t0:t1])

@@ -119,9 +119,6 @@ def tile_moe_shr_glu_relu_kernel(
                 in_=x_in[:, t0:t1, :].rearrange("p t j -> p (t j)"),
             )
 
-        def gpsimd_copy(out, in_):
-            nc.gpsimd.tensor_scalar(out, in_, 1.0, 0.0, MULT, ADD)
-
         def cast_pairs(copy, u, t0, t1):
             copy(
                 out=pairs[u][:, t0:t1].bitcast(BF16).rearrange("p (t d) -> p t d", d=2),
@@ -140,24 +137,29 @@ def tile_moe_shr_glu_relu_kernel(
                 in_=grouped[:].rearrange("p s u -> p (s u)").bitcast(BF16),
             )
 
-        def layer1(e, codes, scales, cols):
-            sums = []
-            for tag, words, planes in (("a", w1, s1), ("b", w3, s3)):
-                bank = psum.tile([P, H], F32, name=f"bank_{tag}", tag=tag)
-                nc.tensor.matmul_mx(
-                    out=bank[:],
-                    lhsT=codes[:, cols].bitcast(FP8X4),
-                    lhsT_scale=scales[:, cols],
-                    rhs=words[:, e, :].bitcast(FP4X4),
-                    rhs_scale=planes[:, e, :],
-                    start=True,
-                    stop=True,
-                )
-                sums.append(bank)
-            positive = work.tile([P, H], F32, name="positive")
-            nc.scalar.activation(positive[:], sums[0][:], RELU)
+        def first_product(codes, scales, cols, words, planes, e, tag, bufs):
+            bank = psum.tile([P, H], F32, name="bank_" + tag, tag=tag, bufs=bufs)
+            nc.tensor.matmul_mx(
+                out=bank[:],
+                lhsT=codes[:, cols].bitcast(FP8X4),
+                lhsT_scale=scales[:, cols],
+                rhs=words[:, e, :].bitcast(FP4X4),
+                rhs_scale=planes[:, e, :],
+                start=True,
+                stop=True,
+            )
+            return bank
+
+        def relu_side(e, codes, scales, cols):
+            bank = first_product(codes, scales, cols, w1, s1, e, "a", 2)
+            positive = work.tile([P, H], F32, name="positive", bufs=9)
+            nc.scalar.activation(positive[:], bank[:], RELU)
+            return positive
+
+        def factor_side(e, codes, scales, cols, positive):
+            bank = first_product(codes, scales, cols, w3, s3, e, "b", 3)
             hidden = work.tile([P, H], BF16, name="hidden", align_bytes=64)
-            nc.vector.tensor_tensor(hidden[:], sums[1][:], positive[:], MULT)
+            nc.vector.tensor_tensor(hidden[:], bank[:], positive[:], MULT)
             return hidden
 
         def turn(group):
@@ -193,7 +195,7 @@ def tile_moe_shr_glu_relu_kernel(
             codes = work.tile([P, n, C], U32, name="h_codes", align_bytes=64)
             scales = work.tile([P, n, C], U8, name="h_scales", align_bytes=64)
             quantize_hidden(turned, codes[:].rearrange("p n c -> p (n c)"), scales[:].rearrange("p n c -> p (n c)"))
-            bank = psum.tile([P, HALVES, n * C], F32, name="bank_y", tag="y")
+            bank = psum.tile([P, HALVES, n * C], F32, name="bank_y", tag="y", bufs=1)
             for i in range(n):
                 for h in range(HALVES):
                     layer2(e0 + i, h, bank[:, h, i * C : (i + 1) * C], codes[:, i, :], scales[:, i, :])
@@ -219,11 +221,18 @@ def tile_moe_shr_glu_relu_kernel(
         ys = {}
         total = chunks + E
 
-        def chunk_step(c):
+        positive = {}
+
+        def where(c):
             if c < chunks:
-                hidden[c] = layer1(SHARED, x_codes, x_scales, cols(c))
-            else:
-                hidden[c] = layer1(c - chunks, g_codes, g_scales, cols(c - chunks))
+                return SHARED, x_codes, x_scales, cols(c)
+            return c - chunks, g_codes, g_scales, cols(c - chunks)
+
+        def a_step(c):
+            positive[c] = relu_side(*where(c))
+
+        def b_step(c):
+            hidden[c] = factor_side(*where(c), positive[c])
 
         def finish(g):
             c, n = groups[g]
@@ -236,38 +245,47 @@ def tile_moe_shr_glu_relu_kernel(
         lay_shared(nc.vector.tensor_copy, 128, 256)
         quantize_shared(0, 128)
         quantize_shared(128, 256)
-        cast_pairs(nc.scalar.copy, 0, 0, 256)
-        cast_pairs(nc.scalar.copy, 1, 0, 256)
-        cast_pairs(nc.scalar.copy, 0, 256, 640)
+        cast_pairs(nc.vector.tensor_copy, 0, 0, 256)
+        cast_pairs(nc.vector.tensor_copy, 1, 0, 256)
+        cast_pairs(nc.vector.tensor_copy, 0, 256, 640)
         cast_pairs(nc.vector.tensor_copy, 1, 256, 640)
+        a_step(0)
+        a_step(1)
         lay_shared(nc.vector.tensor_copy, 256, 640)
-        gather(0, 256)
-        gather(256, 512)
         quantize_shared(256, 512)
         quantize_shared(512, 640)
-        chunk_step(0)
-        chunk_step(1)
-        chunk_step(5)
-        chunk_step(6)
+        gather(0, 256)
+        gather(256, 512)
+        a_step(2)
+        a_step(3)
+        a_step(4)
+        b_step(0)
+        b_step(1)
+        a_step(5)
+        b_step(5)
+        a_step(6)
+        b_step(6)
         turned[0] = turn([hidden[0], hidden[1]])
+        a_step(7)
+        b_step(7)
         turned[3] = turn([hidden[5], hidden[6]])
-        chunk_step(7)
-        chunk_step(8)
-        finish(3)
+        a_step(8)
+        b_step(8)
         finish(0)
+        finish(3)
         turned[4] = turn([hidden[7], hidden[8]])
+        b_step(2)
         finish(4)
-        chunk_step(2)
-        chunk_step(3)
+        b_step(3)
         turned[1] = turn([hidden[2], hidden[3]])
-        chunk_step(4)
+        b_step(4)
         turned[2] = turn([hidden[4]])
         finish(1)
         finish(2)
         tail = psum.tile([P, HALVES, P], F32, name="bank_tail", tag="a")
         bodies = []
         for h in range(HALVES):
-            body = psum.tile([P, 512], F32, name="bank_body", tag="b")
+            body = psum.tile([P, 512], F32, name="bank_body", tag="b", bufs=3)
             layer2(SHARED, h, body[:], hs_codes[:, 0:512], hs_scales[:, 0:512])
             layer2(SHARED, h, tail[:, h, :], hs_codes[:, 512:640], hs_scales[:, 512:640])
             bodies.append(body)

from contextlib import ExitStack

import concourse.mybir as mybir
from concourse.masks import make_identity

FLOPS = 1509949440

K, T, E, C, H, N = 512, 640, 4, 128, 512, 256
S = E * C
SHARED = E
P = 128
HALVES = N // P

F32 = mybir.dt.float32
BF16 = mybir.dt.bfloat16
I32 = mybir.dt.int32
U32 = mybir.dt.uint32
U16 = mybir.dt.uint16
U8 = mybir.dt.uint8
FP8X4 = mybir.dt.float8_e4m3fn_x4
FP4X4 = mybir.dt.float4_e2m1fn_x4
RELU = mybir.ActivationFunctionType.Relu
MULT = mybir.AluOpType.mult
ADD = mybir.AluOpType.add

X_SPLIT = 256


def tile_moe_shr_glu_relu_kernel(
    tc, xT, w1_words, w1_scales, w3_words, w3_scales, w2_words, w2_scales, gate, offs, out
):
    nc = tc.nc
    with ExitStack() as ctx:
        keep = ctx.enter_context(tc.tile_pool(name="keep", bufs=1))
        work = ctx.enter_context(tc.tile_pool(name="work", bufs=6))
        psum = ctx.enter_context(tc.psum_pool(name="psum", bufs=2))

        offsets = keep.tile([P, S // 16], U16, name="offsets")
        x_a = keep.tile([P, 4, X_SPLIT], F32, name="x_a")
        x_b = keep.tile([P, 4, T - X_SPLIT], F32, name="x_b")
        w1 = keep.tile([P, E + 1, 2 * H], U8, name="w1", align_bytes=64)
        w3 = keep.tile([P, E + 1, 2 * H], U8, name="w3", align_bytes=64)
        w2 = keep.tile([P, E + 1, 2 * N], U8, name="w2", align_bytes=64)
        s1 = keep.tile([P, E + 1, H], U8, name="s1", align_bytes=64)
        s3 = keep.tile([P, E + 1, H], U8, name="s3", align_bytes=64)
        s2 = keep.tile([P, E + 1, N], U8, name="s2", align_bytes=64)
        gates = keep.tile([P, HALVES, S], F32, name="gates")
        ident = keep.tile([P, P], F32, name="ident")
        warm = keep.tile([P, 1], F32, name="warm")
        pairs = [keep.tile([P, T], U32, name=f"pairs{u}") for u in range(2)]
        x_in = keep.tile([P, T, 4], BF16, name="x_in", align_bytes=64)
        x_codes = keep.tile([P, T], U32, name="x_codes", align_bytes=64)
        x_scales = keep.tile([P, T], U8, name="x_scales", align_bytes=64)
        g_codes = keep.tile([P, S], U32, name="g_codes", align_bytes=64)
        g_scales = keep.tile([P, S], U8, name="g_scales", align_bytes=64)
        hs_codes = keep.tile([P, T], U32, name="hs_codes", align_bytes=64)
        hs_scales = keep.tile([P, T], U8, name="hs_scales", align_bytes=64)
        windows = [keep.tile([P, T], F32, name=f"window{h}") for h in range(HALVES)]
        results = [keep.tile([P, T], F32, name=f"result{h}") for h in range(HALVES)]

        x_rows = xT.rearrange("(p j) t -> p j t", j=4)

        def load_words(eng, tile, words, e0, e1):
            eng.dma_start(
                out=tile[:, e0:e1, :].bitcast(I32),
                in_=words[e0:e1, 0].rearrange("e p b -> p e b").bitcast(I32),
            )

        def load_scales(eng, tile, scales, r):
            rows = scales[:, 0].rearrange("e (q r) c -> r q e c", r=4)
            eng.dma_start(out=tile[r:P:32, :, :].bitcast(I32), in_=rows[r].bitcast(I32))

        def zero_plane(eng, tile):
            eng.memset(tile[:].rearrange("p e c -> p (e c)").bitcast(I32), 0)

        def touch(words):
            nc.gpsimd.memset(words.bitcast(I32), 0)

        nc.sync.dma_start(out=x_a[:], in_=x_rows[:, :, :X_SPLIT])
        load_words(nc.sync, w1, w1_words, SHARED, SHARED + 1)
        nc.sync.dma_start(offsets[:], offs)
        zero_plane(nc.gpsimd, s1)
        for r in range(4):
            load_scales(nc.sync, s1, w1_scales, r)
        touch(x_b[:, 0, 0:1])
        nc.sync.dma_start(out=x_b[:], in_=x_rows[:, :, X_SPLIT:])
        touch(w3[:, SHARED, 0:4])
        load_words(nc.sync, w3, w3_words, SHARED, SHARED + 1)
        zero_plane(nc.gpsimd, s3)
        for r in range(4):
            load_scales(nc.sync, s3, w3_scales, r)
        touch(w1[:, 0, 0:4])
        load_words(nc.sync, w1, w1_words, 0, E)
        touch(w3[:, 0, 0:4])
        load_words(nc.sync, w3, w3_words, 0, E)
        zero_plane(nc.gpsimd, s2)
        for r in range(4):
            load_scales(nc.sync, s2, w2_scales, r)
        touch(w2[:, 0, 0:4])
        load_words(nc.sync, w2, w2_words, 0, E + 1)
        touch(gates[:, 0, 0:1])
        nc.sync.dma_start(out=gates[:], in_=gate.rearrange("(h p) s -> p h s", p=P))
        make_identity(nc, ident[:])
        nc.vector.memset(warm[:], 0.0)
        nc.scalar.activation(warm[:], warm[:], RELU)
        for h in range(HALVES):
            nc.vector.memset(windows[h][:], 0.0)

        def x_part(t0, t1):
            return x_a[:, :, t0:t1] if t1 <= X_SPLIT else x_b[:, :, t0 - X_SPLIT : t1 - X_SPLIT]

        def lay_shared(eng_copy, t0, t1):
            eng_copy(out=x_in[:, t0:t1, :], in_=x_part(t0, t1).rearrange("p j t -> p t j"))

        def quantize_shared(t0, t1):
            nc.vector.quantize_mx(
                out=x_codes[:, t0:t1].bitcast(FP8X4),
                scales=x_scales[:, t0:t1],
                in_=x_in[:, t0:t1, :].rearrange("p t j -> p (t j)"),
            )

        def cast_pairs(copy, u, t0, t1):
            copy(
                out=pairs[u][:, t0:t1].bitcast(BF16).rearrange("p (t d) -> p t d", d=2),
                in_=x_part(t0, t1)[:, 2 * u : 2 * u + 2, :].rearrange("p d t -> p t d"),
            )

        def gather(j0, j1):
            grouped = work.tile([P, j1 - j0, 2], U32, name="grouped", align_bytes=64)
            for u in range(2):
                nc.vector.tensor_copy(
                    out=grouped[:, :, u], in_=pairs[u][:].indirect(offsets[:, j0 // 16 : j1 // 16])
                )
            nc.vector.quantize_mx(
                out=g_codes[:, j0:j1].bitcast(FP8X4),
                scales=g_scales[:, j0:j1],
                in_=grouped[:].rearrange("p s u -> p (s u)").bitcast(BF16),
            )

        def first_product(codes, scales, cols, words, planes, e, tag, bufs):
            bank = psum.tile([P, H], F32, name="bank_" + tag, tag=tag, bufs=bufs)
            nc.tensor.matmul_mx(
                out=bank[:],
                lhsT=codes[:, cols].bitcast(FP8X4),
                lhsT_scale=scales[:, cols],
                rhs=words[:, e, :].bitcast(FP4X4),
                rhs_scale=planes[:, e, :],
                start=True,
                stop=True,
            )
            return bank

        def relu_side(e, codes, scales, cols):
            bank = first_product(codes, scales, cols, w1, s1, e, "a", 2)
            positive = work.tile([P, H], F32, name="positive", bufs=9)
            nc.scalar.activation(positive[:], bank[:], RELU)
            return positive

        def factor_side(e, codes, scales, cols, positive):
            bank = first_product(codes, scales, cols, w3, s3, e, "b", 3)
            hidden = work.tile([P, H], BF16, name="hidden", align_bytes=64)
            nc.vector.tensor_tensor(hidden[:], bank[:], positive[:], MULT)
            return hidden

        def turn(group):
            n = len(group)
            bank = psum.tile([P, n, 2, P], F32, name="bank_t", tag="t")
            for i, hidden in enumerate(group):
                words = hidden[:].bitcast(F32)
                for u in range(2):
                    nc.tensor.transpose(bank[:, i, u, :], words[:, u::2], ident[:])
            turned = work.tile([P, n, P, 2], F32, name="turned", align_bytes=64)
            nc.scalar.copy(out=turned[:], in_=bank[:].rearrange("p i u r -> p i r u"))
            return turned

        def quantize_hidden(turned, codes, scales):
            nc.vector.quantize_mx(
                out=codes.bitcast(FP8X4),
                scales=scales,
                in_=turned[:].rearrange("p i r u -> p (i r u)").bitcast(BF16),
            )

        def layer2(e, h, bank, codes, scales):
            nc.tensor.matmul_mx(
                out=bank,
                lhsT=w2[:, e, 2 * P * h : 2 * P * (h + 1)].bitcast(FP4X4),
                lhsT_scale=s2[:, e, P * h : P * (h + 1)],
                rhs=codes.bitcast(FP8X4),
                rhs_scale=scales,
                start=True,
                stop=True,
            )

        def experts_out(e0, n, turned):
            codes = work.tile([P, n, C], U32, name="h_codes", align_bytes=64)
            scales = work.tile([P, n, C], U8, name="h_scales", align_bytes=64)
            quantize_hidden(turned, codes[:].rearrange("p n c -> p (n c)"), scales[:].rearrange("p n c -> p (n c)"))
            bank = psum.tile([P, HALVES, n * C], F32, name="bank_y", tag="y", bufs=1)
            for i in range(n):
                for h in range(HALVES):
                    layer2(e0 + i, h, bank[:, h, i * C : (i + 1) * C], codes[:, i, :], scales[:, i, :])
            y = work.tile([P, HALVES, n * C], F32, name="y")
            nc.scalar.copy(out=y[:], in_=bank[:])
            return y

        def scatter(e0, n, h, y):
            nc.vector.tensor_tensor(
                windows[h][:].indirect(offsets[:, e0 * C // 16 : (e0 + n) * C // 16]),
                y[:, h, :],
                gates[:, h, e0 * C : (e0 + n) * C],
                MULT,
            )

        def cols(i, n=1):
            return slice(i * P, (i + n) * P)

        chunks = T // P
        groups = [(0, 2), (2, 2), (4, 1), (5, 2), (7, 2)]
        hidden = {}
        turned = {}
        ys = {}
        total = chunks + E

        positive = {}

        def where(c):
            if c < chunks:
                return SHARED, x_codes, x_scales, cols(c)
            return c - chunks, g_codes, g_scales, cols(c - chunks)

        def a_step(c):
            positive[c] = relu_side(*where(c))

        def b_step(c):
            hidden[c] = factor_side(*where(c), positive[c])

        def finish(g):
            c, n = groups[g]
            if c < chunks:
                quantize_hidden(turned[g], hs_codes[:, cols(c, n)], hs_scales[:, cols(c, n)])
            else:
                ys[g] = experts_out(c - chunks, n, turned[g])

        lay_shared(nc.vector.tensor_copy, 0, 128)
        lay_shared(nc.vector.tensor_copy, 128, 256)
        quantize_shared(0, 128)
        quantize_shared(128, 256)
        cast_pairs(nc.vector.tensor_copy, 0, 0, 256)
        cast_pairs(nc.vector.tensor_copy, 1, 0, 256)
        cast_pairs(nc.vector.tensor_copy, 0, 256, 640)
        cast_pairs(nc.vector.tensor_copy, 1, 256, 640)
        a_step(0)
        a_step(1)
        lay_shared(nc.vector.tensor_copy, 256, 640)
        quantize_shared(256, 512)
        quantize_shared(512, 640)
        gather(0, 256)
        gather(256, 512)
        a_step(2)
        a_step(3)
        a_step(4)
        b_step(0)
        b_step(1)
        a_step(5)
        b_step(5)
        a_step(6)
        b_step(6)
        turned[0] = turn([hidden[0], hidden[1]])
        a_step(7)
        b_step(7)
        turned[3] = turn([hidden[5], hidden[6]])
        a_step(8)
        b_step(8)
        finish(0)
        finish(3)
        turned[4] = turn([hidden[7], hidden[8]])
        b_step(2)
        finish(4)
        b_step(3)
        turned[1] = turn([hidden[2], hidden[3]])
        b_step(4)
        turned[2] = turn([hidden[4]])
        finish(1)
        finish(2)
        tail = psum.tile([P, HALVES, P], F32, name="bank_tail", tag="a")
        bodies = []
        for h in range(HALVES):
            body = psum.tile([P, 512], F32, name="bank_body", tag="b", bufs=3)
            layer2(SHARED, h, body[:], hs_codes[:, 0:512], hs_scales[:, 0:512])
            layer2(SHARED, h, tail[:, h, :], hs_codes[:, 512:640], hs_scales[:, 512:640])
            bodies.append(body)
        for h in range(HALVES):
            scatter(0, 2, h, ys[3])
            scatter(2, 2, h, ys[4])
            for bank, t0, t1 in ((bodies[h][:], 0, 512), (tail[:, h, :], 512, 640)):
                nc.vector.tensor_tensor(results[h][:, t0:t1], bank, windows[h][:, t0:t1], ADD)
                nc.sync.dma_start(out=out[h * P : (h + 1) * P, t0:t1], in_=results[h][:, t0:t1])
